import numpy as np
import ml_dtypes


def mxq(x, axis, fmt="e4m3"):
    dtype, down = {"e4m3": (ml_dtypes.float8_e4m3fn, 7), "e5m2": (ml_dtypes.float8_e5m2, 14)}[fmt]
    v = np.moveaxis(np.asarray(x, np.float32).astype(ml_dtypes.bfloat16).astype(np.float64), axis, -1)
    blocks = v.reshape(v.shape[:-1] + (-1, 32))
    amax = np.abs(blocks).max(-1, keepdims=True)
    byte = np.maximum(np.where(amax > 0, np.frexp(amax)[1] - 1 + 127, 0) - down, 1)
    scale = np.exp2(byte - 127.0)
    codes = (blocks / scale).astype(np.float32).astype(dtype).astype(np.float64)
    return np.moveaxis((codes * scale).reshape(v.shape), -1, axis)


WIDE = False


def mx_kscale(k):
    if not WIDE:
        return np.ones(k)
    levels = np.array([10, -10, 5, -5, 0])
    if k % 512:
        return np.exp2(np.random.permutation(np.resize(levels, k // 32))).repeat(32)
    a = np.empty((k // 512, 16))
    for p in range(k // 512):
        a[p, :8] = np.random.permutation(np.resize(levels, 8))
        for g in range(8):
            far = levels[np.abs(levels - a[p, g]) >= 10]
            a[p, g + 8] = far[np.random.randint(len(far))]
    return np.exp2(a.ravel()).repeat(32)


def f64(x):
    return np.asarray(x).astype(np.float64)


def striped8(idx):
    return np.asarray(idx).reshape(8, -1, 16).transpose(0, 2, 1).reshape(128, -1).astype(np.uint16)


def unstriped8(offs):
    return offs.reshape(8, 16, -1).transpose(0, 2, 1).reshape(8, -1).astype(np.int64)


def pick8(x, idx, run):
    r = np.arange(len(x))
    return x[r[:, None], idx[r % (8 * run) // run]]


E2M1 = np.array([0.0, 0.5, 1.0, 1.5, 2.0, 3.0, 4.0, 6.0, -0.0, -0.5, -1.0, -1.5, -2.0, -3.0, -4.0, -6.0])


def pack_weight(w, fmt):
    k, n = w.shape
    w = f64(np.asarray(w, np.float32).astype(ml_dtypes.bfloat16)).reshape(k // 32, 32, n)
    amax = np.abs(w).max(1)
    if fmt == "e4m3":
        byte = np.frexp(amax)[1] - 1 + 127 - 7
    else:
        mant, ex = np.frexp(amax / 6.0)
        byte = np.where(mant > 0.5, ex, ex - 1) + 127
    byte = np.clip(np.where(amax > 0, byte, 1), 1, 254)
    scaled = (w * np.exp2(127.0 - byte)[:, None, :]).reshape(k, n).astype(np.float32)
    by_word = np.ascontiguousarray(scaled.reshape(k // 512, 128, 4, n).transpose(0, 1, 3, 2))
    if fmt == "e4m3":
        words = by_word.astype(ml_dtypes.float8_e4m3fn).view(np.uint8)
    else:
        c = by_word.astype(ml_dtypes.float4_e2m1fn).view(np.uint8) & 0xF
        words = (c[..., 0::2] | (c[..., 1::2] << 4)).reshape(k // 512, 128, 2 * n)
    return np.ascontiguousarray(words), np.ascontiguousarray(byte.astype(np.uint8).reshape(k // 512, 16, n))


def unpack_weight(words, scales, fmt):
    g, _, n = scales.shape
    words = np.ascontiguousarray(words).reshape(g, 128, n, -1)
    if fmt == "e4m3":
        vals = words.view(ml_dtypes.float8_e4m3fn).astype(np.float64)
    else:
        nib = np.empty((g, 128, n, 4), np.uint8)
        nib[..., 0::2] = words & 0xF
        nib[..., 1::2] = words >> 4
        vals = E2M1[nib]
    vals = vals * np.repeat(np.exp2(scales.astype(np.float64) - 127.0), 8, axis=1)[..., None]
    return vals.transpose(0, 1, 3, 2).reshape(g * 512, n)


D, T, U, I, Q, E = 512, 1024, 1024, 512, 512, 256


def setup_inputs():
    n = np.random.standard_normal
    idx = np.stack([np.random.permutation(T)[:I] for _ in range(8)])
    idx2 = np.stack([np.random.permutation(U)[:I] for _ in range(8)])
    idx3 = np.stack([np.random.permutation(T)[:I] for _ in range(8)])
    idx4 = np.stack([np.random.permutation(U)[:I] for _ in range(8)])
    fd = mx_kscale(D)
    fq = mx_kscale(Q)
    keysp = pack_weight(n((D, T)) / fd[:, None], "e2m1")
    notesp = pack_weight(n((D, U)) / fd[:, None], "e4m3")
    mixp = pack_weight(n((Q, E)) * 1.0 / np.sqrt(Q) / fq[:, None], "e4m3")
    return {
        "query": (n((D, Q)) * 1.0 / np.sqrt(D) * fd[:, None]).astype(np.float32),
        "query2": (n((D, Q)) * 1.0 / np.sqrt(D) * fd[:, None]).astype(np.float32),
        "keys_words": keysp[0],
        "keys_scales": keysp[1],
        "notes_words": notesp[0],
        "notes_scales": notesp[1],
        "rowf": (np.random.uniform(0.5, 2.0, (Q, 1)) * fq[:, None]).astype(np.float32),
        "mix_words": mixp[0],
        "mix_scales": mixp[1],
        "offs": striped8(idx),
        "offs2": striped8(idx2),
        "offs3": striped8(idx3),
        "offs4": striped8(idx4),
    }


def reference(query, query2, keys_words, keys_scales, notes_words, notes_scales, rowf, mix_words, mix_scales, offs, offs2, offs3, offs4):
    idx = unstriped8(offs)
    idx2 = unstriped8(offs2)
    idx3 = unstriped8(offs3)
    idx4 = unstriped8(offs4)
    keysu = unpack_weight(keys_words, keys_scales, "e2m1")
    notesu = unpack_weight(notes_words, notes_scales, "e4m3")
    mixu = unpack_weight(mix_words, mix_scales, "e4m3")
    queryq = mxq(f64(query), 0, "e4m3")
    a = queryq.T @ keysu
    query2q = mxq(f64(query2), 0, "e4m3")
    b = query2q.T @ notesu
    w = np.minimum(pick8(a, idx, 64), pick8(b, idx2, 64))
    f1 = np.zeros((Q, T))
    f1[np.arange(Q)[:, None], idx[np.arange(Q) % 512 // 64]] = w
    f2 = np.zeros((Q, U))
    f2[np.arange(Q)[:, None], idx2[np.arange(Q) % 512 // 64]] = w
    a2 = a - f1
    b2 = b - f2
    g = np.maximum(pick8(a2, idx3, 64), pick8(b2, idx4, 64))
    gw = g * f64(rowf)
    gwq = mxq(gw, 0, "e4m3")
    y = mixu.T @ gwq
    return y

@@ -1,0 +1,211 @@
+from contextlib import ExitStack
+
+import concourse.mybir as mybir
+
+D, T, U, I, Q, E = 512, 1024, 1024, 512, 512, 256
+FLOPS = 2 * D * Q * T + 2 * D * Q * U + 2 * Q * E * I
+
+F32 = mybir.dt.float32
+BF16 = mybir.dt.bfloat16
+I32 = mybir.dt.int32
+U32 = mybir.dt.uint32
+U16 = mybir.dt.uint16
+U8 = mybir.dt.uint8
+FP8X4 = mybir.dt.float8_e4m3fn_x4
+FP4X4 = mybir.dt.float4_e2m1fn_x4
+ALU = mybir.AluOpType
+COPY = mybir.ActivationFunctionType.Copy
+
+P = 128
+PACK = 4
+BANK = 512
+LIST_COLS = I // 16
+
+
+def tile_attend_toppled_twoq_mixed_kernel(tc, query, query2, keys_words, keys_scales, notes_words, notes_scales,
+                                           rowf, mix_words, mix_scales, offs, offs2, offs3, offs4, out):
+    nc = tc.nc
+    with ExitStack() as ctx:
+        lists = ctx.enter_context(tc.tile_pool(name="lists", bufs=1))
+        sb = ctx.enter_context(tc.tile_pool(name="sb", bufs=1))
+        psum = ctx.enter_context(tc.psum_pool(name="psum", bufs=1))
+
+        key_scale = sb.tile([P, T], U8, align_bytes=64)
+        note_scale = sb.tile([P, U], U8, align_bytes=64)
+        mix_scale = sb.tile([P, E], U8, align_bytes=64)
+        for plane in (key_scale, note_scale, mix_scale):
+            nc.vector.memset(plane[:].bitcast(I32), 0)
+        f1 = sb.tile([P, T], F32)
+        f2 = sb.tile([P, U], F32)
+        nc.vector.memset(f1[:], 0.0)
+        nc.vector.memset(f2[:], 0.0)
+
+        def load_scales(plane, scales):
+            for quad in range(4):
+                nc.sync.dma_start(plane[32 * quad : 32 * quad + 4, :].bitcast(I32),
+                                  scales[0, 4 * quad : 4 * quad + 4, :].bitcast(I32))
+
+        def load_list(name, dram):
+            tile = lists.tile([P, LIST_COLS], U16, name=name)
+            nc.sync.dma_start(tile[:], dram)
+            return tile
+
+        q_raw = sb.tile([P, PACK, Q], F32)
+        nc.sync.dma_start(q_raw[:], query.rearrange("(p j) q -> p j q", j=PACK))
+        list1 = load_list("list1", offs)
+        key_words = sb.tile([P, 2 * T], U8, align_bytes=64)
+        nc.sync.dma_start(key_words[:].bitcast(I32), keys_words[0].bitcast(I32))
+        load_scales(key_scale, keys_scales)
+        q2_rows = query2.rearrange("(p j) q -> p j q", j=PACK)
+        q2_raw = []
+        for half in range(2):
+            tile = sb.tile([P, PACK, Q // 2], F32, name="q2_raw%d" % half)
+            nc.sync.dma_start(tile[:], q2_rows[:, :, half * (Q // 2) : (half + 1) * (Q // 2)])
+            q2_raw.append(tile)
+        load_scales(note_scale, notes_scales)
+        note_words = sb.tile([P, U], U32, align_bytes=64)
+        nc.sync.dma_start(note_words[:].bitcast(I32), notes_words[0].rearrange("p n t -> p (n t)").bitcast(I32))
+        list2 = load_list("list2", offs2)
+        list3 = load_list("list3", offs3)
+        list4 = load_list("list4", offs4)
+        factors = sb.tile([P, PACK], F32)
+        nc.sync.dma_start(factors[:], rowf.rearrange("(p r) o -> p (r o)", r=PACK))
+        mix_codes = sb.tile([P, E], U32, align_bytes=64)
+        nc.sync.dma_start(mix_codes[:].bitcast(I32), mix_words[0].rearrange("p n t -> p (n t)").bitcast(I32))
+        load_scales(mix_scale, mix_scales)
+
+        def deal(dealt, raw):
+            nc.vector.tensor_copy(dealt.rearrange("p r m j -> p m j r"),
+                                  raw.rearrange("p j (m r) -> p m j r", r=PACK))
+
+        q_bf = sb.tile([P, PACK, P, PACK], BF16, align_bytes=64)
+        q_codes = sb.tile([P, Q], U32, align_bytes=64)
+        q_scale = sb.tile([P, Q], U8, align_bytes=64)
+        deal(q_bf[:], q_raw[:])
+        nc.vector.quantize_mx(q_codes[:].bitcast(FP8X4), q_scale[:], q_bf[:].rearrange("p r m j -> p (r m j)"))
+
+        q2_bf = sb.tile([P, PACK, P, PACK], BF16, align_bytes=64)
+        q2_codes = sb.tile([P, Q], U32, align_bytes=64)
+        q2_scale = sb.tile([P, Q], U8, align_bytes=64)
+        for half in range(2):
+            deal(q2_bf[:, :, half * (P // 2) : (half + 1) * (P // 2), :], q2_raw[half][:])
+        for lo, hi in ((0, 1), (1, 2), (2, 4)):
+            nc.vector.quantize_mx(q2_codes[:, lo * P : hi * P].bitcast(FP8X4), q2_scale[:, lo * P : hi * P],
+                                  q2_bf[:, lo:hi].rearrange("p r m j -> p (r m j)"))
+
+        def scores(name, r, banks, codes, scale, moving, moving_scale, first_on_vector):
+            table = sb.tile([P, T], F32, name="%s%d" % (name, r))
+            rows = slice(r * P, (r + 1) * P)
+            for half in range(2):
+                cols = slice(half * BANK, (half + 1) * BANK)
+                acc = psum.tile([P, BANK], F32, name="%s%d" % (banks, half))
+                nc.tensor.matmul_mx(acc[:], lhsT=codes[:, rows].bitcast(FP8X4), lhsT_scale=scale[:, rows],
+                                    rhs=moving(half), rhs_scale=moving_scale[:, cols], start=True, stop=True)
+                if half == 0 and first_on_vector:
+                    nc.vector.tensor_copy(table[:, cols], acc[:])
+                else:
+                    nc.scalar.copy(table[:, cols], acc[:])
+            return table
+
+        def key_half(half):
+            return key_words[:, half * 2 * BANK : (half + 1) * 2 * BANK].bitcast(FP4X4)
+
+        def note_half(half):
+            return note_words[:, half * BANK : (half + 1) * BANK].bitcast(FP8X4)
+
+        def look_up(name, table, offsets):
+            picked = sb.tile([P, I], F32, name=name)
+            nc.scalar.activation(picked[:], table[:].indirect(offsets[:]), COPY)
+            return picked
+
+        a, b, a_picked, b_picked, x, y, a2, b2, g = {}, {}, {}, {}, {}, {}, {}, {}, {}
+        gw = sb.tile([P, I, PACK], BF16, align_bytes=64)
+
+        def both_scores(r):
+            a[r] = scores("a", r, "bank_y", q_codes, q_scale, key_half, key_scale, False)
+            b[r] = scores("b", r, "bank_x", q2_codes, q2_scale, note_half, note_scale, False)
+
+        def first_look_ups(r):
+            a_picked[r] = look_up("a_picked%d" % r, a[r], list1)
+            b_picked[r] = look_up("b_picked%d" % r, b[r], list2)
+
+        def lower(r):
+            w = sb.tile([P, I], F32, name="w")
+            nc.vector.tensor_tensor(w[:], a_picked[r][:], b_picked[r][:], ALU.min)
+            return w
+
+        def topple_a(r, w):
+            nc.vector.tensor_copy(f1[:].indirect(list1[:]), w[:])
+            a2[r] = sb.tile([P, T], F32, name="a2_%d" % r)
+            nc.gpsimd.tensor_tensor(a2[r][:], a[r][:], f1[:], ALU.subtract)
+
+        def scatter_b(w):
+            nc.vector.tensor_copy(f2[:].indirect(list2[:]), w[:])
+
+        def topple_b(r, engine, name):
+            b2[r] = sb.tile([P, U], F32, name=name)
+            engine.tensor_tensor(b2[r][:], b[r][:], f2[:], ALU.subtract)
+
+        def larger(r, name):
+            g[r] = sb.tile([P, I], F32, name=name)
+            nc.vector.tensor_tensor(g[r][:], x[r][:], y[r][:], ALU.max)
+
+        def weigh_on_scalar(r):
+            nc.scalar.activation(gw[:, :, r], g[r][:], COPY, scale=factors[:, r : r + 1])
+
+        def weigh_on_vector(r):
+            nc.vector.tensor_scalar(gw[:, :, r], g[r][:], factors[:, r : r + 1], None, ALU.mult)
+
+        shared = ("shared0", "shared1")
+
+        a[0] = scores("a", 0, "bank_x", q_codes, q_scale, key_half, key_scale, False)
+        a_picked[0] = look_up("a_picked0", a[0], list1)
+        b[0] = scores("b", 0, "bank_y", q2_codes, q2_scale, note_half, note_scale, True)
+        b_picked[0] = sb.tile([P, I], F32, name="b_picked0")
+        nc.vector.tensor_copy(b_picked[0][:, : I // 2], b[0][:].indirect(list2[:, : LIST_COLS // 2]))
+        nc.scalar.activation(b_picked[0][:, I // 2 :], b[0][:].indirect(list2[:, LIST_COLS // 2 :]), COPY)
+
+        last = PACK - 1
+        for r in range(PACK):
+            w = lower(r)
+            if r >= 2:
+                larger(r - 2, "g%d" % (r - 2))
+            if r >= 1:
+                topple_b(r - 1, nc.gpsimd, shared[(r - 1) % 2])
+            if r == 0:
+                both_scores(1)
+            if r < last:
+                first_look_ups(r + 1)
+            if r >= 1:
+                x[r - 1] = look_up("x%d" % (r - 1), a2[r - 1], list3)
+            if r >= 2:
+                weigh_on_scalar(r - 2)
+            if r >= 1:
+                y[r - 1] = look_up(shared[r % 2], b2[r - 1], list4)
+            if r + 2 <= last:
+                both_scores(r + 2)
+            topple_a(r, w)
+            scatter_b(w)
+
+        x[last] = look_up("x%d" % last, a2[last], list3)
+        topple_b(last, nc.vector, "b2_last")
+        y[last] = look_up("y_last", b2[last], list4)
+        larger(last - 1, "b%d" % last)
+        weigh_on_vector(last - 1)
+        larger(last, "g%d" % last)
+        weigh_on_vector(last)
+
+        gw_codes = sb.tile([P, I], U32, align_bytes=64)
+        gw_scale = sb.tile([P, I], U8, align_bytes=64)
+        nc.vector.quantize_mx(gw_codes[:].bitcast(FP8X4), gw_scale[:], gw[:].rearrange("p i r -> p (i r)"))
+        for half in range(2):
+            rows = slice(half * P, (half + 1) * P)
+            acc = psum.tile([P, BANK], F32, name="bank_x%d" % half)
+            nc.tensor.matmul_mx(acc[:], lhsT=mix_codes[:, rows].bitcast(FP8X4), lhsT_scale=mix_scale[:, rows],
+                                rhs=gw_codes[:].bitcast(FP8X4), rhs_scale=gw_scale[:], start=True, stop=True)
+            result = sb.tile([P, I], F32, name="result%d" % half)
+            if half == 0:
+                nc.scalar.copy(result[:], acc[:])
+            else:
+                nc.vector.tensor_copy(result[:], acc[:])
+            nc.sync.dma_start(out[rows, :], result[:])

@@ -50,18 +50,21 @@ def tile_attend_toppled_twoq_mixed_kernel(tc, query, query2, keys_words, keys_sc
             nc.sync.dma_start(tile[:], dram)
             return tile
 
-        q_raw = sb.tile([P, PACK, Q], F32)
-        nc.sync.dma_start(q_raw[:], query.rearrange("(p j) q -> p j q", j=PACK))
+        def load_queries(name, dram):
+            rows = dram.rearrange("(p j) q -> p j q", j=PACK)
+            halves = []
+            for half in range(2):
+                tile = sb.tile([P, PACK, Q // 2], F32, name="%s%d" % (name, half))
+                nc.sync.dma_start(tile[:], rows[:, :, half * (Q // 2) : (half + 1) * (Q // 2)])
+                halves.append(tile)
+            return halves
+
+        q_raw = load_queries("q_raw", query)
         list1 = load_list("list1", offs)
         key_words = sb.tile([P, 2 * T], U8, align_bytes=64)
         nc.sync.dma_start(key_words[:].bitcast(I32), keys_words[0].bitcast(I32))
         load_scales(key_scale, keys_scales)
-        q2_rows = query2.rearrange("(p j) q -> p j q", j=PACK)
-        q2_raw = []
-        for half in range(2):
-            tile = sb.tile([P, PACK, Q // 2], F32, name="q2_raw%d" % half)
-            nc.sync.dma_start(tile[:], q2_rows[:, :, half * (Q // 2) : (half + 1) * (Q // 2)])
-            q2_raw.append(tile)
+        q2_raw = load_queries("q2_raw", query2)
         load_scales(note_scale, notes_scales)
         note_words = sb.tile([P, U], U32, align_bytes=64)
         nc.sync.dma_start(note_words[:].bitcast(I32), notes_words[0].rearrange("p n t -> p (n t)").bitcast(I32))
@@ -81,7 +84,8 @@ def tile_attend_toppled_twoq_mixed_kernel(tc, query, query2, keys_words, keys_sc
         q_bf = sb.tile([P, PACK, P, PACK], BF16, align_bytes=64)
         q_codes = sb.tile([P, Q], U32, align_bytes=64)
         q_scale = sb.tile([P, Q], U8, align_bytes=64)
-        deal(q_bf[:], q_raw[:])
+        for half in range(2):
+            deal(q_bf[:, :, half * (P // 2) : (half + 1) * (P // 2), :], q_raw[half][:])
         nc.vector.quantize_mx(q_codes[:].bitcast(FP8X4), q_scale[:], q_bf[:].rearrange("p r m j -> p (r m j)"))
 
         q2_bf = sb.tile([P, PACK, P, PACK], BF16, align_bytes=64)
@@ -119,7 +123,7 @@ def tile_attend_toppled_twoq_mixed_kernel(tc, query, query2, keys_words, keys_sc
             return picked
 
         a, b, a_picked, b_picked, x, y, a2, b2, g = {}, {}, {}, {}, {}, {}, {}, {}, {}
-        gw = sb.tile([P, I, PACK], BF16, align_bytes=64)
+        gw = [sb.tile([P, I // 2, PACK], BF16, align_bytes=64, name="gw%d" % half) for half in range(2)]
 
         def both_scores(r):
             a[r] = scores("a", r, "bank_y", q_codes, q_scale, key_half, key_scale, False)
@@ -127,10 +131,9 @@ def tile_attend_toppled_twoq_mixed_kernel(tc, query, query2, keys_words, keys_sc
 
         def first_look_ups(r):
             a_picked[r] = look_up("a_picked%d" % r, a[r], list1)
-            b_picked[r] = look_up("b_picked%d" % r, b[r], list2)
 
         def lower(r):
-            w = sb.tile([P, I], F32, name="w")
+            w = sb.tile([P, I], F32, name="w%d" % r)
             nc.vector.tensor_tensor(w[:], a_picked[r][:], b_picked[r][:], ALU.min)
             return w
 
@@ -151,12 +154,9 @@ def tile_attend_toppled_twoq_mixed_kernel(tc, query, query2, keys_words, keys_sc
             nc.vector.tensor_tensor(g[r][:], x[r][:], y[r][:], ALU.max)
 
         def weigh_on_scalar(r):
-            nc.scalar.activation(gw[:, :, r], g[r][:], COPY, scale=factors[:, r : r + 1])
-
-        def weigh_on_vector(r):
-            nc.vector.tensor_scalar(gw[:, :, r], g[r][:], factors[:, r : r + 1], None, ALU.mult)
-
-        shared = ("shared0", "shared1")
+            for half in range(2):
+                nc.scalar.activation(gw[half][:, :, r], g[r][:, half * (I // 2) : (half + 1) * (I // 2)], COPY,
+                                     scale=factors[:, r : r + 1])
 
         a[0] = scores("a", 0, "bank_x", q_codes, q_scale, key_half, key_scale, False)
         a_picked[0] = look_up("a_picked0", a[0], list1)
@@ -167,21 +167,23 @@ def tile_attend_toppled_twoq_mixed_kernel(tc, query, query2, keys_words, keys_sc
 
         last = PACK - 1
         for r in range(PACK):
-            w = lower(r)
             if r >= 2:
                 larger(r - 2, "g%d" % (r - 2))
+            w = lower(r)
             if r >= 1:
-                topple_b(r - 1, nc.gpsimd, shared[(r - 1) % 2])
+                topple_b(r - 1, nc.gpsimd, "chain")
             if r == 0:
                 both_scores(1)
+            if r >= 1:
+                x[r - 1] = look_up("x%d" % (r - 1), a2[r - 1], list3)
             if r < last:
                 first_look_ups(r + 1)
             if r >= 1:
-                x[r - 1] = look_up("x%d" % (r - 1), a2[r - 1], list3)
+                y[r - 1] = look_up("y%d" % (r - 1), b2[r - 1], list4)
+            if r < last:
+                b_picked[r + 1] = look_up("chain", b[r + 1], list2)
             if r >= 2:
                 weigh_on_scalar(r - 2)
-            if r >= 1:
-                y[r - 1] = look_up(shared[r % 2], b2[r - 1], list4)
             if r + 2 <= last:
                 both_scores(r + 2)
             topple_a(r, w)
@@ -189,23 +191,27 @@ def tile_attend_toppled_twoq_mixed_kernel(tc, query, query2, keys_words, keys_sc
 
         x[last] = look_up("x%d" % last, a2[last], list3)
         topple_b(last, nc.vector, "b2_last")
-        y[last] = look_up("y_last", b2[last], list4)
         larger(last - 1, "b%d" % last)
-        weigh_on_vector(last - 1)
-        larger(last, "g%d" % last)
-        weigh_on_vector(last)
-
-        gw_codes = sb.tile([P, I], U32, align_bytes=64)
-        gw_scale = sb.tile([P, I], U8, align_bytes=64)
-        nc.vector.quantize_mx(gw_codes[:].bitcast(FP8X4), gw_scale[:], gw[:].rearrange("p i r -> p (i r)"))
-        for half in range(2):
-            rows = slice(half * P, (half + 1) * P)
-            acc = psum.tile([P, BANK], F32, name="bank_x%d" % half)
-            nc.tensor.matmul_mx(acc[:], lhsT=mix_codes[:, rows].bitcast(FP8X4), lhsT_scale=mix_scale[:, rows],
-                                rhs=gw_codes[:].bitcast(FP8X4), rhs_scale=gw_scale[:], start=True, stop=True)
-            result = sb.tile([P, I], F32, name="result%d" % half)
-            if half == 0:
-                nc.scalar.copy(result[:], acc[:])
-            else:
-                nc.vector.tensor_copy(result[:], acc[:])
-            nc.sync.dma_start(out[rows, :], result[:])
+        halves = [slice(half * (I // 2), (half + 1) * (I // 2)) for half in range(2)]
+        for half, slots in enumerate(halves):
+            y_half = sb.tile([P, I // 2], F32, name="y_last%d" % half)
+            nc.scalar.activation(
+                y_half[:], b2[last][:].indirect(list4[:, half * (LIST_COLS // 2) : (half + 1) * (LIST_COLS // 2)]), COPY)
+            g_half = sb.tile([P, I // 2], F32, name="g_last%d" % half)
+            nc.vector.tensor_tensor(g_half[:], x[last][:, slots], y_half[:], ALU.max)
+            nc.vector.tensor_scalar(gw[half][:, :, last - 1], g[last - 1][:, slots], factors[:, last - 1 : last], None, ALU.mult)
+            nc.vector.tensor_scalar(gw[half][:, :, last], g_half[:], factors[:, last : last + 1], None, ALU.mult)
+            gw_codes = sb.tile([P, I // 2], U32, align_bytes=64, name="gw_codes%d" % half)
+            gw_scale = sb.tile([P, I // 2], U8, align_bytes=64, name="gw_scale%d" % half)
+            nc.vector.quantize_mx(gw_codes[:].bitcast(FP8X4), gw_scale[:], gw[half][:].rearrange("p i r -> p (i r)"))
+            result = sb.tile([P, E // P, I // 2], F32, name="result%d" % half)
+            for c in range(E // P):
+                rows = slice(c * P, (c + 1) * P)
+                acc = psum.tile([P, I // 2], F32, name="%s%d" % (("bank_x", "bank_y")[half], c))
+                nc.tensor.matmul_mx(acc[:], lhsT=mix_codes[:, rows].bitcast(FP8X4), lhsT_scale=mix_scale[:, rows],
+                                    rhs=gw_codes[:].bitcast(FP8X4), rhs_scale=gw_scale[:], start=True, stop=True)
+                if half == 1 and c == 1:
+                    nc.vector.tensor_copy(result[:, c, :], acc[:])
+                else:
+                    nc.scalar.copy(result[:, c, :], acc[:])
+            nc.sync.dma_start(out.rearrange("(c p) i -> p c i", p=P)[:, :, slots], result[:])

@@ -50,24 +50,22 @@ def tile_attend_toppled_twoq_mixed_kernel(tc, query, query2, keys_words, keys_sc
             nc.sync.dma_start(tile[:], dram)
             return tile
 
-        def load_queries(name, dram):
-            rows = dram.rearrange("(p j) q -> p j q", j=PACK)
-            halves = []
-            for half in range(2):
-                tile = sb.tile([P, PACK, Q // 2], F32, name="%s%d" % (name, half))
-                nc.sync.dma_start(tile[:], rows[:, :, half * (Q // 2) : (half + 1) * (Q // 2)])
-                halves.append(tile)
-            return halves
-
-        q_raw = load_queries("q_raw", query)
+        q_raw = sb.tile([P, PACK, Q], F32)
+        nc.sync.dma_start(q_raw[:], query.rearrange("(p j) q -> p j q", j=PACK))
         list1 = load_list("list1", offs)
         key_words = sb.tile([P, 2 * T], U8, align_bytes=64)
         nc.sync.dma_start(key_words[:].bitcast(I32), keys_words[0].bitcast(I32))
         load_scales(key_scale, keys_scales)
-        q2_raw = load_queries("q2_raw", query2)
+        q2_raw = sb.tile([P, PACK, Q], F32)
+        for j in (0, 2):
+            nc.sync.dma_start(q2_raw[:, j : j + 2, :], query2.rearrange("(p j) q -> p j q", j=PACK)[:, j : j + 2, :])
         load_scales(note_scale, notes_scales)
-        note_words = sb.tile([P, U], U32, align_bytes=64)
-        nc.sync.dma_start(note_words[:].bitcast(I32), notes_words[0].rearrange("p n t -> p (n t)").bitcast(I32))
+        note_words = []
+        for half in range(2):
+            tile = sb.tile([P, BANK], U32, align_bytes=64, name="note_words%d" % half)
+            words = notes_words[0, :, half * BANK : (half + 1) * BANK, :].rearrange("p n t -> p (n t)")
+            nc.sync.dma_start(tile[:].bitcast(I32), words.bitcast(I32))
+            note_words.append(tile)
         list2 = load_list("list2", offs2)
         list3 = load_list("list3", offs3)
         list4 = load_list("list4", offs4)
@@ -77,60 +75,61 @@ def tile_attend_toppled_twoq_mixed_kernel(tc, query, query2, keys_words, keys_sc
         nc.sync.dma_start(mix_codes[:].bitcast(I32), mix_words[0].rearrange("p n t -> p (n t)").bitcast(I32))
         load_scales(mix_scale, mix_scales)
 
-        def deal(dealt, raw):
-            nc.vector.tensor_copy(dealt.rearrange("p r m j -> p m j r"),
-                                  raw.rearrange("p j (m r) -> p m j r", r=PACK))
+        def deal(copy, dealt, raw, first, places):
+            copy(dealt[:, :, :, places].rearrange("p r m j -> p m j r"),
+                 raw[:, places, :].rearrange("p j (m r) -> p m j r", r=PACK)[:, :, :, first : first + 2])
 
-        q_bf = sb.tile([P, PACK, P, PACK], BF16, align_bytes=64)
-        q_codes = sb.tile([P, Q], U32, align_bytes=64)
-        q_scale = sb.tile([P, Q], U8, align_bytes=64)
-        for half in range(2):
-            deal(q_bf[:, :, half * (P // 2) : (half + 1) * (P // 2), :], q_raw[half][:])
-        nc.vector.quantize_mx(q_codes[:].bitcast(FP8X4), q_scale[:], q_bf[:].rearrange("p r m j -> p (r m j)"))
+        def quantise(name, dealt):
+            width = dealt.shape[1] // PACK
+            codes = sb.tile([P, width], U32, align_bytes=64, name="%s_codes" % name)
+            scale = sb.tile([P, width], U8, align_bytes=64, name="%s_scale" % name)
+            nc.vector.quantize_mx(codes[:].bitcast(FP8X4), scale[:], dealt)
+            return [(codes[:, c : c + P], scale[:, c : c + P]) for c in range(0, width, P)]
 
-        q2_bf = sb.tile([P, PACK, P, PACK], BF16, align_bytes=64)
-        q2_codes = sb.tile([P, Q], U32, align_bytes=64)
-        q2_scale = sb.tile([P, Q], U8, align_bytes=64)
-        for half in range(2):
-            deal(q2_bf[:, :, half * (P // 2) : (half + 1) * (P // 2), :], q2_raw[half][:])
-        for lo, hi in ((0, 1), (1, 2), (2, 4)):
-            nc.vector.quantize_mx(q2_codes[:, lo * P : hi * P].bitcast(FP8X4), q2_scale[:, lo * P : hi * P],
-                                  q2_bf[:, lo:hi].rearrange("p r m j -> p (r m j)"))
+        def quantise_early(name, dealt):
+            return [quantise("%s%d" % (name, r), dealt[:, r].rearrange("p m j -> p (m j)"))[0] for r in range(2)]
 
-        def scores(name, r, banks, codes, scale, moving, moving_scale, first_on_vector):
-            table = sb.tile([P, T], F32, name="%s%d" % (name, r))
-            rows = slice(r * P, (r + 1) * P)
+        def quantise_late(name, dealt):
+            return quantise("%s_late" % name, dealt[:].rearrange("p r m j -> p (r m j)"))
+
+        q_early, q_late, q2_early, q2_late = [
+            sb.tile([P, 2, P, PACK], BF16, align_bytes=64, name=name)
+            for name in ("q_early", "q_late", "q2_early", "q2_late")]
+        deal(nc.vector.tensor_copy, q_early, q_raw, 0, slice(0, PACK))
+        deal(nc.scalar.copy, q_late, q_raw, 2, slice(0, PACK))
+        q_mx = quantise_early("q", q_early) + quantise_late("q", q_late)
+        deal(nc.vector.tensor_copy, q2_early, q2_raw, 0, slice(0, 2))
+        deal(nc.vector.tensor_copy, q2_late, q2_raw, 2, slice(0, 2))
+        deal(nc.vector.tensor_copy, q2_early, q2_raw, 0, slice(2, PACK))
+        q2_mx = quantise_early("q2", q2_early)
+        deal(nc.vector.tensor_copy, q2_late, q2_raw, 2, slice(2, PACK))
+        q2_mx.extend(quantise_late("q2", q2_late))
+
+        def scores(name, r, banks, rows_mx, moving, moving_scale, first_copy=nc.scalar.copy):
+            codes, scale = rows_mx[r]
+            table = sb.tile([P, T], F32, align_bytes=64, name="%s%d" % (name, r))
             for half in range(2):
                 cols = slice(half * BANK, (half + 1) * BANK)
-                acc = psum.tile([P, BANK], F32, name="%s%d" % (banks, half))
-                nc.tensor.matmul_mx(acc[:], lhsT=codes[:, rows].bitcast(FP8X4), lhsT_scale=scale[:, rows],
+                acc = psum.tile([P, BANK], F32, name=banks[half])
+                nc.tensor.matmul_mx(acc[:], lhsT=codes.bitcast(FP8X4), lhsT_scale=scale,
                                     rhs=moving(half), rhs_scale=moving_scale[:, cols], start=True, stop=True)
-                if half == 0 and first_on_vector:
-                    nc.vector.tensor_copy(table[:, cols], acc[:])
-                else:
-                    nc.scalar.copy(table[:, cols], acc[:])
+                (first_copy if half == 0 else nc.scalar.copy)(table[:, cols], acc[:])
             return table
 
         def key_half(half):
             return key_words[:, half * 2 * BANK : (half + 1) * 2 * BANK].bitcast(FP4X4)
 
         def note_half(half):
-            return note_words[:, half * BANK : (half + 1) * BANK].bitcast(FP8X4)
+            return note_words[half][:].bitcast(FP8X4)
 
         def look_up(name, table, offsets):
-            picked = sb.tile([P, I], F32, name=name)
+            picked = sb.tile([P, I], F32, align_bytes=64, name=name)
             nc.scalar.activation(picked[:], table[:].indirect(offsets[:]), COPY)
             return picked
 
         a, b, a_picked, b_picked, x, y, a2, b2, g = {}, {}, {}, {}, {}, {}, {}, {}, {}
         gw = [sb.tile([P, I // 2, PACK], BF16, align_bytes=64, name="gw%d" % half) for half in range(2)]
 
-        def both_scores(r):
-            a[r] = scores("a", r, "bank_y", q_codes, q_scale, key_half, key_scale, False)
-            b[r] = scores("b", r, "bank_x", q2_codes, q2_scale, note_half, note_scale, False)
-
-        def first_look_ups(r):
-            a_picked[r] = look_up("a_picked%d" % r, a[r], list1)
 
         def lower(r):
             w = sb.tile([P, I], F32, name="w%d" % r)
@@ -146,7 +145,7 @@ def tile_attend_toppled_twoq_mixed_kernel(tc, query, query2, keys_words, keys_sc
             nc.vector.tensor_copy(f2[:].indirect(list2[:]), w[:])
 
         def topple_b(r, engine, name):
-            b2[r] = sb.tile([P, U], F32, name=name)
+            b2[r] = sb.tile([P, U], F32, align_bytes=64, name=name)
             engine.tensor_tensor(b2[r][:], b[r][:], f2[:], ALU.subtract)
 
         def larger(r, name):
@@ -158,9 +157,9 @@ def tile_attend_toppled_twoq_mixed_kernel(tc, query, query2, keys_words, keys_sc
                 nc.scalar.activation(gw[half][:, :, r], g[r][:, half * (I // 2) : (half + 1) * (I // 2)], COPY,
                                      scale=factors[:, r : r + 1])
 
-        a[0] = scores("a", 0, "bank_x", q_codes, q_scale, key_half, key_scale, False)
-        a_picked[0] = look_up("a_picked0", a[0], list1)
-        b[0] = scores("b", 0, "bank_y", q2_codes, q2_scale, note_half, note_scale, True)
+        a[0] = scores("a", 0, ("bank_x0", "bank_x1"), q_mx, key_half, key_scale)
+        a_picked[0] = look_up("b1", a[0], list1)
+        b[0] = scores("b", 0, ("bank_y0", "bank_y1"), q2_mx, note_half, note_scale, nc.vector.tensor_copy)
         b_picked[0] = sb.tile([P, I], F32, name="b_picked0")
         nc.vector.tensor_copy(b_picked[0][:, : I // 2], b[0][:].indirect(list2[:, : LIST_COLS // 2]))
         nc.scalar.activation(b_picked[0][:, I // 2 :], b[0][:].indirect(list2[:, LIST_COLS // 2 :]), COPY)
@@ -172,26 +171,25 @@ def tile_attend_toppled_twoq_mixed_kernel(tc, query, query2, keys_words, keys_sc
             w = lower(r)
             if r >= 1:
                 topple_b(r - 1, nc.gpsimd, "chain")
-            if r == 0:
-                both_scores(1)
+            if r < last:
+                a[r + 1] = scores("a", r + 1, ("bank_y1", "bank_y1"), q_mx, key_half, key_scale)
             if r >= 1:
                 x[r - 1] = look_up("x%d" % (r - 1), a2[r - 1], list3)
             if r < last:
-                first_look_ups(r + 1)
+                a_picked[r + 1] = look_up("a_picked%d" % (r + 1), a[r + 1], list1)
+                b[r + 1] = scores("b", r + 1, ("bank_x0", "bank_x1"), q2_mx, note_half, note_scale)
             if r >= 1:
                 y[r - 1] = look_up("y%d" % (r - 1), b2[r - 1], list4)
             if r < last:
                 b_picked[r + 1] = look_up("chain", b[r + 1], list2)
             if r >= 2:
                 weigh_on_scalar(r - 2)
-            if r + 2 <= last:
-                both_scores(r + 2)
             topple_a(r, w)
             scatter_b(w)
 
         x[last] = look_up("x%d" % last, a2[last], list3)
         topple_b(last, nc.vector, "b2_last")
-        larger(last - 1, "b%d" % last)
+        larger(last - 1, "g%d" % (last - 1))
         halves = [slice(half * (I // 2), (half + 1) * (I // 2)) for half in range(2)]
         for half, slots in enumerate(halves):
             y_half = sb.tile([P, I // 2], F32, name="y_last%d" % half)
@@ -204,14 +202,14 @@ def tile_attend_toppled_twoq_mixed_kernel(tc, query, query2, keys_words, keys_sc
             gw_codes = sb.tile([P, I // 2], U32, align_bytes=64, name="gw_codes%d" % half)
             gw_scale = sb.tile([P, I // 2], U8, align_bytes=64, name="gw_scale%d" % half)
             nc.vector.quantize_mx(gw_codes[:].bitcast(FP8X4), gw_scale[:], gw[half][:].rearrange("p i r -> p (i r)"))
-            result = sb.tile([P, E // P, I // 2], F32, name="result%d" % half)
             for c in range(E // P):
                 rows = slice(c * P, (c + 1) * P)
                 acc = psum.tile([P, I // 2], F32, name="%s%d" % (("bank_x", "bank_y")[half], c))
                 nc.tensor.matmul_mx(acc[:], lhsT=mix_codes[:, rows].bitcast(FP8X4), lhsT_scale=mix_scale[:, rows],
                                     rhs=gw_codes[:].bitcast(FP8X4), rhs_scale=gw_scale[:], start=True, stop=True)
+                result = sb.tile([P, I // 2], F32, name="result%d%d" % (half, c))
                 if half == 1 and c == 1:
-                    nc.vector.tensor_copy(result[:, c, :], acc[:])
+                    nc.vector.tensor_copy(result[:], acc[:])
                 else:
-                    nc.scalar.copy(result[:, c, :], acc[:])
-            nc.sync.dma_start(out.rearrange("(c p) i -> p c i", p=P)[:, :, slots], result[:])
+                    nc.scalar.copy(result[:], acc[:])
+                nc.sync.dma_start(out[rows, slots], result[:])

@@ -128,7 +128,7 @@ def tile_attend_toppled_twoq_mixed_kernel(tc, query, query2, keys_words, keys_sc
             return picked
 
         a, b, a_picked, b_picked, x, y, a2, b2, g = {}, {}, {}, {}, {}, {}, {}, {}, {}
-        gw = [sb.tile([P, I // 2, PACK], BF16, align_bytes=64, name="gw%d" % half) for half in range(2)]
+        gw = []
 
 
         def lower(r):
@@ -166,11 +166,14 @@ def tile_attend_toppled_twoq_mixed_kernel(tc, query, query2, keys_words, keys_sc
 
         last = PACK - 1
         for r in range(PACK):
+            w = lower(r)
             if r >= 2:
                 larger(r - 2, "g%d" % (r - 2))
-            w = lower(r)
             if r >= 1:
-                topple_b(r - 1, nc.gpsimd, "chain")
+                topple_b(r - 1, nc.gpsimd, "b_picked1" if r == 1 else "y%d" % (r - 2))
+            if r == last:
+                gw.extend(sb.tile([P, I // 2, PACK], BF16, align_bytes=64, name=tag) for tag in ("a_picked3", "x1"))
+                weigh_on_scalar(0)
             if r < last:
                 a[r + 1] = scores("a", r + 1, ("bank_y1", "bank_y1"), q_mx, key_half, key_scale)
             if r >= 1:
@@ -178,12 +181,11 @@ def tile_attend_toppled_twoq_mixed_kernel(tc, query, query2, keys_words, keys_sc
             if r < last:
                 a_picked[r + 1] = look_up("a_picked%d" % (r + 1), a[r + 1], list1)
                 b[r + 1] = scores("b", r + 1, ("bank_x0", "bank_x1"), q2_mx, note_half, note_scale)
+                b_picked[r + 1] = look_up("b_picked1" if r == 0 else "b%d" % (r - 1), b[r + 1], list2)
             if r >= 1:
                 y[r - 1] = look_up("y%d" % (r - 1), b2[r - 1], list4)
-            if r < last:
-                b_picked[r + 1] = look_up("chain", b[r + 1], list2)
-            if r >= 2:
-                weigh_on_scalar(r - 2)
+            if r == last:
+                weigh_on_scalar(1)
             topple_a(r, w)
             scatter_b(w)
 

from contextlib import ExitStack

import concourse.mybir as mybir

D, T, U, I, Q, E = 512, 1024, 1024, 512, 512, 256
FLOPS = 2 * D * Q * T + 2 * D * Q * U + 2 * Q * E * I

F32 = mybir.dt.float32
BF16 = mybir.dt.bfloat16
I32 = mybir.dt.int32
U32 = mybir.dt.uint32
U16 = mybir.dt.uint16
U8 = mybir.dt.uint8
FP8X4 = mybir.dt.float8_e4m3fn_x4
FP4X4 = mybir.dt.float4_e2m1fn_x4
ALU = mybir.AluOpType
COPY = mybir.ActivationFunctionType.Copy

P = 128
PACK = 4
BANK = 512
LIST_COLS = I // 16


def tile_attend_toppled_twoq_mixed_kernel(tc, query, query2, keys_words, keys_scales, notes_words, notes_scales,
                                           rowf, mix_words, mix_scales, offs, offs2, offs3, offs4, out):
    nc = tc.nc
    with ExitStack() as ctx:
        lists = ctx.enter_context(tc.tile_pool(name="lists", bufs=1))
        sb = ctx.enter_context(tc.tile_pool(name="sb", bufs=1))
        psum = ctx.enter_context(tc.psum_pool(name="psum", bufs=1))

        key_scale = sb.tile([P, T], U8, align_bytes=64)
        note_scale = sb.tile([P, U], U8, align_bytes=64)
        mix_scale = sb.tile([P, E], U8, align_bytes=64)
        for plane in (key_scale, note_scale, mix_scale):
            nc.vector.memset(plane[:].bitcast(I32), 0)
        f1 = sb.tile([P, T], F32)
        f2 = sb.tile([P, U], F32)
        nc.vector.memset(f1[:], 0.0)
        nc.vector.memset(f2[:], 0.0)

        def load_scales(plane, scales):
            for quad in range(4):
                nc.sync.dma_start(plane[32 * quad : 32 * quad + 4, :].bitcast(I32),
                                  scales[0, 4 * quad : 4 * quad + 4, :].bitcast(I32))

        def load_list(name, dram):
            tile = lists.tile([P, LIST_COLS], U16, name=name)
            nc.sync.dma_start(tile[:], dram)
            return tile

        q_raw = sb.tile([P, PACK, Q], F32)
        nc.sync.dma_start(q_raw[:], query.rearrange("(p j) q -> p j q", j=PACK))
        list1 = load_list("list1", offs)
        key_words = sb.tile([P, 2 * T], U8, align_bytes=64)
        nc.sync.dma_start(key_words[:].bitcast(I32), keys_words[0].bitcast(I32))
        load_scales(key_scale, keys_scales)
        q2_raw = sb.tile([P, PACK, Q], F32)
        for j in (0, 2):
            nc.sync.dma_start(q2_raw[:, j : j + 2, :], query2.rearrange("(p j) q -> p j q", j=PACK)[:, j : j + 2, :])
        load_scales(note_scale, notes_scales)
        note_words = []
        for half in range(2):
            tile = sb.tile([P, BANK], U32, align_bytes=64, name="note_words%d" % half)
            words = notes_words[0, :, half * BANK : (half + 1) * BANK, :].rearrange("p n t -> p (n t)")
            nc.sync.dma_start(tile[:].bitcast(I32), words.bitcast(I32))
            note_words.append(tile)
        list2 = load_list("list2", offs2)
        list3 = load_list("list3", offs3)
        list4 = load_list("list4", offs4)
        factors = sb.tile([P, PACK], F32)
        nc.sync.dma_start(factors[:], rowf.rearrange("(p r) o -> p (r o)", r=PACK))
        mix_codes = sb.tile([P, E], U32, align_bytes=64)
        nc.sync.dma_start(mix_codes[:].bitcast(I32), mix_words[0].rearrange("p n t -> p (n t)").bitcast(I32))
        load_scales(mix_scale, mix_scales)

        def deal(copy, dealt, raw, first, places):
            copy(dealt[:, :, :, places].rearrange("p r m j -> p m j r"),
                 raw[:, places, :].rearrange("p j (m r) -> p m j r", r=PACK)[:, :, :, first : first + 2])

        def quantise(name, dealt):
            width = dealt.shape[1] // PACK
            codes = sb.tile([P, width], U32, align_bytes=64, name="%s_codes" % name)
            scale = sb.tile([P, width], U8, align_bytes=64, name="%s_scale" % name)
            nc.vector.quantize_mx(codes[:].bitcast(FP8X4), scale[:], dealt)
            return [(codes[:, c : c + P], scale[:, c : c + P]) for c in range(0, width, P)]

        def quantise_early(name, dealt):
            return [quantise("%s%d" % (name, r), dealt[:, r].rearrange("p m j -> p (m j)"))[0] for r in range(2)]

        def quantise_late(name, dealt):
            return quantise("%s_late" % name, dealt[:].rearrange("p r m j -> p (r m j)"))

        q_early, q_late, q2_early, q2_late = [
            sb.tile([P, 2, P, PACK], BF16, align_bytes=64, name=name)
            for name in ("q_early", "q_late", "q2_early", "q2_late")]
        deal(nc.vector.tensor_copy, q_early, q_raw, 0, slice(0, PACK))
        deal(nc.scalar.copy, q_late, q_raw, 2, slice(0, PACK))
        q_mx = quantise_early("q", q_early) + quantise_late("q", q_late)
        deal(nc.vector.tensor_copy, q2_early, q2_raw, 0, slice(0, 2))
        deal(nc.vector.tensor_copy, q2_late, q2_raw, 2, slice(0, 2))
        deal(nc.vector.tensor_copy, q2_early, q2_raw, 0, slice(2, PACK))
        q2_mx = quantise_early("q2", q2_early)
        deal(nc.vector.tensor_copy, q2_late, q2_raw, 2, slice(2, PACK))
        q2_mx.extend(quantise_late("q2", q2_late))

        def scores(name, r, banks, rows_mx, moving, moving_scale, first_copy=nc.scalar.copy):
            codes, scale = rows_mx[r]
            table = sb.tile([P, T], F32, align_bytes=64, name="%s%d" % (name, r))
            for half in range(2):
                cols = slice(half * BANK, (half + 1) * BANK)
                acc = psum.tile([P, BANK], F32, name=banks[half])
                nc.tensor.matmul_mx(acc[:], lhsT=codes.bitcast(FP8X4), lhsT_scale=scale,
                                    rhs=moving(half), rhs_scale=moving_scale[:, cols], start=True, stop=True)
                (first_copy if half == 0 else nc.scalar.copy)(table[:, cols], acc[:])
            return table

        def key_half(half):
            return key_words[:, half * 2 * BANK : (half + 1) * 2 * BANK].bitcast(FP4X4)

        def note_half(half):
            return note_words[half][:].bitcast(FP8X4)

        def look_up(name, table, offsets):
            picked = sb.tile([P, I], F32, align_bytes=64, name=name)
            nc.scalar.activation(picked[:], table[:].indirect(offsets[:]), COPY)
            return picked

        a, b, a_picked, b_picked, x, y, a2, b2, g = {}, {}, {}, {}, {}, {}, {}, {}, {}
        gw = []


        def lower(r):
            w = sb.tile([P, I], F32, name="w%d" % r)
            nc.vector.tensor_tensor(w[:], a_picked[r][:], b_picked[r][:], ALU.min)
            return w

        def topple_a(r, w):
            nc.vector.tensor_copy(f1[:].indirect(list1[:]), w[:])
            a2[r] = sb.tile([P, T], F32, name="a2_%d" % r)
            nc.gpsimd.tensor_tensor(a2[r][:], a[r][:], f1[:], ALU.subtract)

        def scatter_b(w):
            nc.vector.tensor_copy(f2[:].indirect(list2[:]), w[:])

        def topple_b(r, engine, name):
            b2[r] = sb.tile([P, U], F32, align_bytes=64, name=name)
            engine.tensor_tensor(b2[r][:], b[r][:], f2[:], ALU.subtract)

        def larger(r, name):
            g[r] = sb.tile([P, I], F32, name=name)
            nc.vector.tensor_tensor(g[r][:], x[r][:], y[r][:], ALU.max)

        def weigh_on_scalar(r):
            for half in range(2):
                nc.scalar.activation(gw[half][:, :, r], g[r][:, half * (I // 2) : (half + 1) * (I // 2)], COPY,
                                     scale=factors[:, r : r + 1])

        a[0] = scores("a", 0, ("bank_x0", "bank_x1"), q_mx, key_half, key_scale)
        a_picked[0] = look_up("b1", a[0], list1)
        b[0] = scores("b", 0, ("bank_y0", "bank_y1"), q2_mx, note_half, note_scale, nc.vector.tensor_copy)
        b_picked[0] = sb.tile([P, I], F32, name="b_picked0")
        nc.vector.tensor_copy(b_picked[0][:, : I // 2], b[0][:].indirect(list2[:, : LIST_COLS // 2]))
        nc.scalar.activation(b_picked[0][:, I // 2 :], b[0][:].indirect(list2[:, LIST_COLS // 2 :]), COPY)

        last = PACK - 1
        for r in range(PACK):
            w = lower(r)
            if r >= 2:
                larger(r - 2, "g%d" % (r - 2))
            if r >= 1:
                topple_b(r - 1, nc.gpsimd, "b_picked1" if r == 1 else "y%d" % (r - 2))
            if r == last:
                gw.extend(sb.tile([P, I // 2, PACK], BF16, align_bytes=64, name=tag) for tag in ("a_picked3", "x1"))
                weigh_on_scalar(0)
            if r < last:
                a[r + 1] = scores("a", r + 1, ("bank_y1", "bank_y1"), q_mx, key_half, key_scale)
            if r >= 1:
                x[r - 1] = look_up("x%d" % (r - 1), a2[r - 1], list3)
            if r < last:
                a_picked[r + 1] = look_up("a_picked%d" % (r + 1), a[r + 1], list1)
                b[r + 1] = scores("b", r + 1, ("bank_x0", "bank_x1"), q2_mx, note_half, note_scale)
                b_picked[r + 1] = look_up("b_picked1" if r == 0 else "b%d" % (r - 1), b[r + 1], list2)
            if r >= 1:
                y[r - 1] = look_up("y%d" % (r - 1), b2[r - 1], list4)
            if r == last:
                weigh_on_scalar(1)
            topple_a(r, w)
            scatter_b(w)

        x[last] = look_up("x%d" % last, a2[last], list3)
        topple_b(last, nc.vector, "b2_last")
        larger(last - 1, "g%d" % (last - 1))
        halves = [slice(half * (I // 2), (half + 1) * (I // 2)) for half in range(2)]
        for half, slots in enumerate(halves):
            y_half = sb.tile([P, I // 2], F32, name="y_last%d" % half)
            nc.scalar.activation(
                y_half[:], b2[last][:].indirect(list4[:, half * (LIST_COLS // 2) : (half + 1) * (LIST_COLS // 2)]), COPY)
            g_half = sb.tile([P, I // 2], F32, name="g_last%d" % half)
            nc.vector.tensor_tensor(g_half[:], x[last][:, slots], y_half[:], ALU.max)
            nc.vector.tensor_scalar(gw[half][:, :, last - 1], g[last - 1][:, slots], factors[:, last - 1 : last], None, ALU.mult)
            nc.vector.tensor_scalar(gw[half][:, :, last], g_half[:], factors[:, last : last + 1], None, ALU.mult)
            gw_codes = sb.tile([P, I // 2], U32, align_bytes=64, name="gw_codes%d" % half)
            gw_scale = sb.tile([P, I // 2], U8, align_bytes=64, name="gw_scale%d" % half)
            nc.vector.quantize_mx(gw_codes[:].bitcast(FP8X4), gw_scale[:], gw[half][:].rearrange("p i r -> p (i r)"))
            for c in range(E // P):
                rows = slice(c * P, (c + 1) * P)
                acc = psum.tile([P, I // 2], F32, name="%s%d" % (("bank_x", "bank_y")[half], c))
                nc.tensor.matmul_mx(acc[:], lhsT=mix_codes[:, rows].bitcast(FP8X4), lhsT_scale=mix_scale[:, rows],
                                    rhs=gw_codes[:].bitcast(FP8X4), rhs_scale=gw_scale[:], start=True, stop=True)
                result = sb.tile([P, I // 2], F32, name="result%d%d" % (half, c))
                if half == 1 and c == 1:
                    nc.vector.tensor_copy(result[:], acc[:])
                else:
                    nc.scalar.copy(result[:], acc[:])
                nc.sync.dma_start(out[rows, slots], result[:])
